import numpy as np
import ml_dtypes


def mxq(x, axis, fmt="e4m3"):
    dtype, down = {"e4m3": (ml_dtypes.float8_e4m3fn, 7), "e5m2": (ml_dtypes.float8_e5m2, 14)}[fmt]
    v = np.moveaxis(np.asarray(x, np.float32).astype(ml_dtypes.bfloat16).astype(np.float64), axis, -1)
    blocks = v.reshape(v.shape[:-1] + (-1, 32))
    amax = np.abs(blocks).max(-1, keepdims=True)
    byte = np.maximum(np.where(amax > 0, np.frexp(amax)[1] - 1 + 127, 0) - down, 1)
    scale = np.exp2(byte - 127.0)
    codes = (blocks / scale).astype(np.float32).astype(dtype).astype(np.float64)
    return np.moveaxis((codes * scale).reshape(v.shape), -1, axis)


WIDE = False


def mx_kscale(k):
    if not WIDE:
        return np.ones(k)
    levels = np.array([10, -10, 5, -5, 0])
    if k % 512:
        return np.exp2(np.random.permutation(np.resize(levels, k // 32))).repeat(32)
    a = np.empty((k // 512, 16))
    for p in range(k // 512):
        a[p, :8] = np.random.permutation(np.resize(levels, 8))
        for g in range(8):
            far = levels[np.abs(levels - a[p, g]) >= 10]
            a[p, g + 8] = far[np.random.randint(len(far))]
    return np.exp2(a.ravel()).repeat(32)


def f64(x):
    return np.asarray(x).astype(np.float64)


def striped(idx):
    return np.tile(np.asarray(idx).reshape(-1, 16).T, (8, 1)).astype(np.uint16)


def unstriped(offs):
    return offs[:16].T.reshape(-1).astype(np.int64)


E2M1 = np.array([0.0, 0.5, 1.0, 1.5, 2.0, 3.0, 4.0, 6.0, -0.0, -0.5, -1.0, -1.5, -2.0, -3.0, -4.0, -6.0])


def pack_weight(w, fmt):
    k, n = w.shape
    w = f64(np.asarray(w, np.float32).astype(ml_dtypes.bfloat16)).reshape(k // 32, 32, n)
    amax = np.abs(w).max(1)
    if fmt == "e4m3":
        byte = np.frexp(amax)[1] - 1 + 127 - 7
    else:
        mant, ex = np.frexp(amax / 6.0)
        byte = np.where(mant > 0.5, ex, ex - 1) + 127
    byte = np.clip(np.where(amax > 0, byte, 1), 1, 254)
    scaled = (w * np.exp2(127.0 - byte)[:, None, :]).reshape(k, n).astype(np.float32)
    by_word = np.ascontiguousarray(scaled.reshape(k // 512, 128, 4, n).transpose(0, 1, 3, 2))
    if fmt == "e4m3":
        words = by_word.astype(ml_dtypes.float8_e4m3fn).view(np.uint8)
    else:
        c = by_word.astype(ml_dtypes.float4_e2m1fn).view(np.uint8) & 0xF
        words = (c[..., 0::2] | (c[..., 1::2] << 4)).reshape(k // 512, 128, 2 * n)
    return np.ascontiguousarray(words), np.ascontiguousarray(byte.astype(np.uint8).reshape(k // 512, 16, n))


def unpack_weight(words, scales, fmt):
    g, _, n = scales.shape
    words = np.ascontiguousarray(words).reshape(g, 128, n, -1)
    if fmt == "e4m3":
        vals = words.view(ml_dtypes.float8_e4m3fn).astype(np.float64)
    else:
        nib = np.empty((g, 128, n, 4), np.uint8)
        nib[..., 0::2] = words & 0xF
        nib[..., 1::2] = words >> 4
        vals = E2M1[nib]
    vals = vals * np.repeat(np.exp2(scales.astype(np.float64) - 127.0), 8, axis=1)[..., None]
    return vals.transpose(0, 1, 3, 2).reshape(g * 512, n)


B, N, T, D, DV, NQ = 1, 2048, 4096, 1024, 256, 128
PAGE = 512
DRAFT = 128


def setup_inputs():
    n = np.random.standard_normal
    pages = np.random.permutation(T // PAGE)[:B * N // PAGE]
    idx = (pages[:, None] * PAGE + np.arange(PAGE)[None, :]).reshape(-1)
    s = mx_kscale(D)[:, None]
    u = np.ones(T)
    u[idx] = mx_kscale(B * N)
    r = np.random.uniform(0.5, 2.0, T)
    qp = [pack_weight(x, "e4m3") for x in n((B, D, NQ)) * s * (1.00 / np.sqrt(D))]
    k = n((D, T)) / s
    v = n((DV, T)) / (u * r)
    kp = pack_weight(k, "e2m1")
    vp = pack_weight(v.T, "e4m3")
    when = np.zeros(T)
    when[idx] = np.concatenate([np.concatenate([np.arange(N - DRAFT), N - DRAFT + np.random.randint(0, 16, DRAFT)]) for b in range(B)])
    return {
        "q_words": np.stack([x[0] for x in qp]),
        "q_scales": np.stack([x[1] for x in qp]),
        "k_words": np.ascontiguousarray(kp[0].reshape(D // 1024, 2, 128, T, 2).transpose(0, 2, 3, 1, 4)).reshape(D // 1024, 128, T, 4),
        "k_scales": kp[1],
        "v_words": vp[0],
        "v_scales": vp[1],
        "vs": np.tile(u * r, (128, 1)).astype(np.float32),
        "pos": np.tile(when, (128, 1)).astype(np.float32),
        "qpos": np.random.randint(N - DRAFT, N - DRAFT + 16, (B, NQ, 1)).astype(np.float32),
        "offs": striped(idx),
        "voffs": striped((pages[:, None] * DV + np.arange(DV)[None, :]).reshape(-1)),
    }


def reference(q_words, q_scales, k_words, k_scales, v_words, v_scales, vs, pos, qpos, offs, voffs):
    idx = unstriped(offs)
    k = unpack_weight(k_words.reshape(D // 1024, 128, T, 2, 2).transpose(0, 3, 1, 2, 4).reshape(D // 512, 128, 2 * T), k_scales, "e2m1")
    v = unpack_weight(v_words, v_scales, "e4m3")
    v = v.reshape(T // 512, 512, DV)[unstriped(voffs)[::DV] // DV].reshape(B, N, DV)
    pick = lambda x: x[:, idx].reshape(x.shape[0], B, N).transpose(1, 0, 2)
    q = np.stack([unpack_weight(q_words[b], q_scales[b], "e4m3") for b in range(B)])
    score = q.transpose(0, 2, 1) @ pick(k)
    score = np.where(pick(f64(pos))[:, :1, :] <= f64(qpos), score, -30000.0)
    m = score.max(-1, keepdims=True)
    p = np.exp(score - m)
    total = p.sum(-1, keepdims=True)
    w = p * pick(f64(vs))[:, :1, :]
    y = mxq(w, 2, "e4m3") @ v
    y = y / total
    return y

@@ -1,0 +1,235 @@
+from contextlib import ExitStack
+
+import concourse.mybir as mybir
+from concourse.masks import make_identity
+
+F32 = mybir.dt.float32
+BF16 = mybir.dt.bfloat16
+I32 = mybir.dt.int32
+U32 = mybir.dt.uint32
+U16 = mybir.dt.uint16
+U8 = mybir.dt.uint8
+FP8X4 = mybir.dt.float8_e4m3fn_x4
+FP4X4 = mybir.dt.float4_e2m1fn_x4
+ALU = mybir.AluOpType
+ACT = mybir.ActivationFunctionType
+AXIS = mybir.AxisListType
+
+P = 128
+NQ, N, T, D, DV = 128, 2048, 4096, 1024, 256
+PAGE = 512
+PAGES = N // PAGE
+POOL_PAGES = T // PAGE
+PACK = 4
+PASSES = D // (P * PACK)
+QUADS = 4
+COLS = PAGE // 16
+MASKED = -30000.0
+OPEN = 2.0 ** 100
+
+FLOPS = 2 * NQ * N * D + 2 * NQ * N * DV
+
+
+def tile_attend_pkv4q_soft_draft_kernel(
+    tc, q_words, q_scales, k_words, k_scales, v_words, v_scales, vs, pos, qpos, offs, voffs, out
+):
+    nc = tc.nc
+    with ExitStack() as ctx:
+        lists = ctx.enter_context(tc.tile_pool(name="lists", bufs=1))
+        keep = ctx.enter_context(tc.tile_pool(name="keep", bufs=1))
+        ring = ctx.enter_context(tc.tile_pool(name="ring", bufs=PAGES))
+        psum = ctx.enter_context(tc.psum_pool(name="psum", bufs=1))
+
+        slots = lists.tile([P, N // 16], U16, name="slots")
+        vcols = lists.tile([P, PAGES * DV // 16], U16, name="vcols")
+
+        ks_pool = keep.tile([P, T], U8, name="ks_pool", tag="ks_then_v", align_bytes=64)
+        vsc_pool = keep.tile([P, POOL_PAGES * DV], U8, name="vsc_pool", align_bytes=64)
+        vs_pool = keep.tile([P, T], F32, name="vs_pool", align_bytes=64)
+        pos_pool = keep.tile([P, T], F32, name="pos_pool", align_bytes=64)
+        kw_pool = keep.tile([P, T], I32, name="kw_pool", align_bytes=64)
+        q_codes = keep.tile([P, PASSES * NQ], I32, name="q_codes", align_bytes=64)
+        q_planes = keep.tile([P, PASSES * NQ], U8, name="q_planes", align_bytes=64)
+        k_planes = keep.tile([P, PASSES * N], U8, name="k_planes", align_bytes=64)
+        qpos_col = keep.tile([P, 1], F32, name="qpos_col")
+        open_col = keep.tile([P, 1], F32, name="open_col")
+        ident = keep.tile([P, P], F32, name="ident", align_bytes=64)
+        warm = keep.tile([P, 1], F32, name="warm")
+
+        ks_row0 = P - PASSES * 16
+        nc.sync.dma_start(slots[:], offs)
+        nc.sync.dma_start(
+            ks_pool[ks_row0:P, :].bitcast(I32), k_scales.rearrange("o f t -> (o f) t").bitcast(I32)
+        )
+        nc.sync.dma_start(vcols[:], voffs)
+        nc.sync.dma_start(pos_pool[:], pos)
+        nc.sync.dma_start(kw_pool[:], k_words[0].rearrange("p t b -> p (t b)").bitcast(I32))
+
+        nc.vector.memset(vsc_pool[:].bitcast(I32), 0)
+        nc.vector.memset(vs_pool[:], 0.0)
+        nc.vector.memset(ks_pool[0:ks_row0, :].bitcast(I32), 0)
+        nc.vector.memset(q_planes[:].bitcast(I32), 0)
+        nc.vector.memset(k_planes[:].bitcast(I32), 0)
+
+        for quad in range(QUADS):
+            nc.scalar.dma_start(
+                vsc_pool[32 * quad : 32 * quad + 4, :].bitcast(I32).rearrange("f (u e) -> f u e", u=POOL_PAGES),
+                v_scales[:, 4 * quad : 4 * quad + 4, :].bitcast(I32).rearrange("u f e -> f u e"),
+            )
+        nc.scalar.dma_start(vs_pool[0:1, :], vs[0:1, :])
+
+        nc.gpsimd.dma_start(qpos_col[:], qpos[0])
+        nc.gpsimd.memset(open_col[:], OPEN)
+        nc.scalar.activation(warm[:], open_col[:], ACT.Exp, scale=-1.0)
+        make_identity(nc, ident[:])
+        nc.gpsimd.dma_start(
+            q_codes[:].rearrange("g (o q) -> g o q", o=PASSES),
+            q_words[0].rearrange("o g q r -> g o (q r)").bitcast(I32),
+        )
+        for quad in range(QUADS):
+            nc.gpsimd.dma_start(
+                q_planes[32 * quad : 32 * quad + 4, :].bitcast(I32).rearrange("f (o q) -> f o q", o=PASSES),
+                q_scales[0, :, 4 * quad : 4 * quad + 4, :].bitcast(I32).rearrange("o f q -> f o q"),
+            )
+
+        ks_got = keep.tile([P, N], U8, name="ks_got", align_bytes=64)
+        nc.vector.tensor_copy(ks_got[:], ks_pool[:].indirect(slots[:]))
+        for o in range(PASSES):
+            for quad in range(QUADS):
+                row = ks_row0 + 16 * o + 4 * quad
+                nc.sync.dma_start(
+                    k_planes[32 * quad : 32 * quad + 4, o * N : (o + 1) * N].bitcast(I32),
+                    ks_got[row : row + 4, :].bitcast(I32),
+                )
+
+        vw_pool = keep.tile([P, POOL_PAGES * DV], I32, name="vw_pool", tag="ks_then_v", align_bytes=64)
+        nc.sync.dma_start(
+            vw_pool[:].rearrange("g (u e) -> g u e", u=POOL_PAGES),
+            v_words.rearrange("u g e r -> g u (e r)").bitcast(I32),
+        )
+
+        v_planes = keep.tile([P, PAGES * DV], U8, name="v_planes", align_bytes=64)
+        nc.vector.tensor_copy(v_planes[:], vsc_pool[:].indirect(vcols[:]))
+
+        vs_got = keep.tile([P, N], F32, name="vs_got", align_bytes=64)
+        nc.vector.tensor_copy(vs_got[:], vs_pool[:].indirect(slots[:]))
+        vs_cols = keep.tile([P, PAGES, PACK], F32, name="vs_cols", align_bytes=64)
+        for page in range(PAGES):
+            turned = psum.tile([P, PACK, P], F32, name="turned", tag="turned", bufs=PAGES)
+            for r in range(PACK):
+                nc.tensor.transpose(
+                    turned[:, r, :], vs_got[:, page * PAGE + r : (page + 1) * PAGE : PACK], ident[:]
+                )
+            nc.scalar.copy(vs_cols[:, page, :], turned[:, :, 0])
+
+        caps = []
+        for page in range(PAGES):
+            page_slots = slots[:, page * COLS : (page + 1) * COLS]
+            pos_got = ring.tile([P, PAGE], F32, name="pos_got", align_bytes=64)
+            nc.vector.tensor_copy(pos_got[:], pos_pool[:].indirect(page_slots))
+            side = ring.tile([P, PACK, P], F32, name="side", align_bytes=64)
+            nc.scalar.activation(
+                side[:].rearrange("q r s -> q s r"),
+                pos_got[:].rearrange("q (s r) -> q s r", r=PACK),
+                ACT.Sign,
+                bias=qpos_col[:],
+                scale=-1.0,
+            )
+            cap = ring.tile([P, PACK, P], F32, name="cap", align_bytes=64)
+            nc.scalar.activation(cap[:], side[:], ACT.Relu, bias=open_col[:], scale=OPEN)
+            caps.append(cap)
+
+        banks = []
+        for page in range(PAGES):
+            page_slots = slots[:, page * COLS : (page + 1) * COLS]
+            kw_got = ring.tile([P, PAGE], U32, name="kw_got", align_bytes=64)
+            nc.vector.tensor_copy(kw_got[:], kw_pool[:].bitcast(U32).indirect(page_slots))
+            k_codes = ring.tile([P, PASSES, PAGE], U16, name="k_codes", align_bytes=64)
+            nc.vector.tensor_copy(k_codes[:], kw_got[:].bitcast(U16).rearrange("g (n o) -> g o n", o=PASSES))
+            scores = psum.tile([P, PAGE], F32, name="scores", tag="scores", bufs=3)
+            for o in range(PASSES):
+                nc.tensor.matmul_mx(
+                    out=scores[:],
+                    lhsT=q_codes[:, o * NQ : (o + 1) * NQ].bitcast(FP8X4),
+                    lhsT_scale=q_planes[:, o * NQ : (o + 1) * NQ],
+                    rhs=k_codes[:, o, :].bitcast(FP4X4),
+                    rhs_scale=k_planes[:, o * N + page * PAGE : o * N + (page + 1) * PAGE],
+                    start=(o == 0),
+                    stop=(o == PASSES - 1),
+                )
+            banks.append(scores)
+
+            if page == PAGES - 1:
+                masked = keep.tile([P, PACK, P], F32, name="masked_last", tag="masked_then_v", align_bytes=64)
+            else:
+                masked = ring.tile([P, PACK, P], F32, name="masked", align_bytes=64)
+            nc.vector.scalar_tensor_tensor(
+                out=masked[:],
+                in0=caps[page][:],
+                scalar=MASKED,
+                in1=scores[:].rearrange("q (s r) -> q r s", r=PACK),
+                op0=ALU.add,
+                op1=ALU.min,
+            )
+            if page == 0:
+                neg_max = keep.tile([P, PAGES], F32, name="neg_max")
+                negated = keep.tile([P, PAGES, PAGE], F32, name="negated", align_bytes=64)
+            nc.vector.tensor_scalar(
+                out=negated[:, page, :],
+                in0=masked[:].rearrange("q r s -> q (r s)"),
+                scalar1=-1.0,
+                scalar2=None if page == 0 else neg_max[:, page - 1 : page],
+                op0=ALU.mult,
+                op1=ALU.min,
+                accum_out=neg_max[:, page : page + 1],
+            )
+
+        v_codes = keep.tile([P, PAGES * DV], U32, name="v_codes", tag="masked_then_v", align_bytes=64)
+        nc.vector.tensor_copy(v_codes[:], vw_pool[:].bitcast(U32).indirect(vcols[:]))
+
+        sums = keep.tile([P, PAGES], F32, name="sums")
+        acc = psum.tile([P, DV], F32, name="acc", tag="acc")
+        for page in range(PAGES):
+            probs = ring.tile([P, PACK, P], F32, name="probs", align_bytes=64)
+            nc.scalar.activation(
+                probs[:].rearrange("q r s -> q (r s)"),
+                negated[:, page, :],
+                ACT.Exp,
+                bias=neg_max[:, PAGES - 1 : PAGES],
+                scale=-1.0,
+                accum_out=sums[:, page : page + 1],
+            )
+            turned = psum.tile([P, PACK, P], F32, name="turned", tag="turned", bufs=PAGES)
+            for r in range(PACK):
+                nc.tensor.transpose(turned[:, r, :], probs[:, r, :], ident[:])
+            weights = ring.tile([P, NQ, PACK], BF16, name="weights", align_bytes=64)
+            nc.vector.tensor_tensor(
+                weights[:],
+                turned[:].rearrange("s r q -> s q r"),
+                vs_cols[:, page, :].unsqueeze(1).broadcast_to([P, NQ, PACK]),
+                ALU.mult,
+            )
+            w_codes = ring.tile([P, NQ], U32, name="w_codes", align_bytes=64)
+            w_plane = ring.tile([P, NQ], U8, name="w_plane", align_bytes=64)
+            nc.vector.quantize_mx(
+                out=w_codes[:].bitcast(FP8X4),
+                scales=w_plane[:],
+                in_=weights[:].rearrange("s q r -> s (q r)"),
+            )
+            nc.tensor.matmul_mx(
+                out=acc[:],
+                lhsT=w_codes[:].bitcast(FP8X4),
+                lhsT_scale=w_plane[:],
+                rhs=v_codes[:, page * DV : (page + 1) * DV].bitcast(FP8X4),
+                rhs_scale=v_planes[:, page * DV : (page + 1) * DV],
+                start=(page == 0),
+                stop=(page == PAGES - 1),
+            )
+
+        total = keep.tile([P, 1], F32, name="total")
+        nc.vector.tensor_reduce(total[:], sums[:], AXIS.X, ALU.add)
+        inverse = keep.tile([P, 1], F32, name="inverse")
+        nc.vector.reciprocal(inverse[:], total[:])
+        result = keep.tile([P, DV], F32, name="result", align_bytes=64)
+        nc.scalar.activation(result[:], acc[:], ACT.Copy, scale=inverse[:])
+        nc.sync.dma_start(out[0], result[:])

@@ -24,7 +24,6 @@ PACK = 4
 PASSES = D // (P * PACK)
 QUADS = 4
 COLS = PAGE // 16
-MASKED = -30000.0
 OPEN = 2.0 ** 100
 
 FLOPS = 2 * NQ * N * D + 2 * NQ * N * DV
@@ -44,15 +43,14 @@ def tile_attend_pkv4q_soft_draft_kernel(
         vcols = lists.tile([P, PAGES * DV // 16], U16, name="vcols")
 
         ks_pool = keep.tile([P, T], U8, name="ks_pool", tag="ks_then_v", align_bytes=64)
-        vsc_pool = keep.tile([P, POOL_PAGES * DV], U8, name="vsc_pool", align_bytes=64)
-        vs_pool = keep.tile([P, T], F32, name="vs_pool", align_bytes=64)
+        vsc_pool = keep.tile([P, POOL_PAGES * DV], U8, name="vsc_pool", tag="vsc_then_v", align_bytes=64)
         pos_pool = keep.tile([P, T], F32, name="pos_pool", align_bytes=64)
         kw_pool = keep.tile([P, T], I32, name="kw_pool", align_bytes=64)
         q_codes = keep.tile([P, PASSES * NQ], I32, name="q_codes", align_bytes=64)
         q_planes = keep.tile([P, PASSES * NQ], U8, name="q_planes", align_bytes=64)
         k_planes = keep.tile([P, PASSES * N], U8, name="k_planes", align_bytes=64)
         qpos_col = keep.tile([P, 1], F32, name="qpos_col")
-        open_col = keep.tile([P, 1], F32, name="open_col")
+        neg_qpos = keep.tile([P, 1], F32, name="neg_qpos")
         ident = keep.tile([P, P], F32, name="ident", align_bytes=64)
         warm = keep.tile([P, 1], F32, name="warm")
 
@@ -66,7 +64,6 @@ def tile_attend_pkv4q_soft_draft_kernel(
         nc.sync.dma_start(kw_pool[:], k_words[0].rearrange("p t b -> p (t b)").bitcast(I32))
 
         nc.vector.memset(vsc_pool[:].bitcast(I32), 0)
-        nc.vector.memset(vs_pool[:], 0.0)
         nc.vector.memset(ks_pool[0:ks_row0, :].bitcast(I32), 0)
         nc.vector.memset(q_planes[:].bitcast(I32), 0)
         nc.vector.memset(k_planes[:].bitcast(I32), 0)
@@ -76,12 +73,11 @@ def tile_attend_pkv4q_soft_draft_kernel(
                 vsc_pool[32 * quad : 32 * quad + 4, :].bitcast(I32).rearrange("f (u e) -> f u e", u=POOL_PAGES),
                 v_scales[:, 4 * quad : 4 * quad + 4, :].bitcast(I32).rearrange("u f e -> f u e"),
             )
-        nc.scalar.dma_start(vs_pool[0:1, :], vs[0:1, :])
 
         nc.gpsimd.dma_start(qpos_col[:], qpos[0])
-        nc.gpsimd.memset(open_col[:], OPEN)
-        nc.scalar.activation(warm[:], open_col[:], ACT.Exp, scale=-1.0)
         make_identity(nc, ident[:])
+        nc.scalar.activation(warm[:], ident[:, 0:1], ACT.Exp)
+        nc.scalar.activation(neg_qpos[:], qpos_col[:], ACT.Copy, scale=-1.0)
         nc.gpsimd.dma_start(
             q_codes[:].rearrange("g (o q) -> g o q", o=PASSES),
             q_words[0].rearrange("o g q r -> g o (q r)").bitcast(I32),
@@ -102,89 +98,99 @@ def tile_attend_pkv4q_soft_draft_kernel(
                     ks_got[row : row + 4, :].bitcast(I32),
                 )
 
-        vw_pool = keep.tile([P, POOL_PAGES * DV], I32, name="vw_pool", tag="ks_then_v", align_bytes=64)
+        vs_pool = keep.tile([P, T], F32, name="vs_pool", tag="ks_then_v", align_bytes=64)
+        nc.sync.dma_start(vs_pool[:], vs)
+
+        v_planes = keep.tile([P, PAGES * DV], U8, name="v_planes", align_bytes=64)
+        nc.vector.tensor_copy(v_planes[:], vsc_pool[:].indirect(vcols[:]))
+
+        vw_pool = keep.tile([P, POOL_PAGES * DV], I32, name="vw_pool", tag="vsc_then_v", align_bytes=64)
         nc.sync.dma_start(
             vw_pool[:].rearrange("g (u e) -> g u e", u=POOL_PAGES),
             v_words.rearrange("u g e r -> g u (e r)").bitcast(I32),
         )
 
-        v_planes = keep.tile([P, PAGES * DV], U8, name="v_planes", align_bytes=64)
-        nc.vector.tensor_copy(v_planes[:], vsc_pool[:].indirect(vcols[:]))
+        def turn(bank_part, rows, start=True, stop=True):
+            nc.tensor.matmul(bank_part, rows, ident[:], start=start, stop=stop, is_transpose=True)
 
-        vs_got = keep.tile([P, N], F32, name="vs_got", align_bytes=64)
-        nc.vector.tensor_copy(vs_got[:], vs_pool[:].indirect(slots[:]))
-        vs_cols = keep.tile([P, PAGES, PACK], F32, name="vs_cols", align_bytes=64)
-        for page in range(PAGES):
-            turned = psum.tile([P, PACK, P], F32, name="turned", tag="turned", bufs=PAGES)
-            for r in range(PACK):
-                nc.tensor.transpose(
-                    turned[:, r, :], vs_got[:, page * PAGE + r : (page + 1) * PAGE : PACK], ident[:]
-                )
-            nc.scalar.copy(vs_cols[:, page, :], turned[:, :, 0])
+        def bank(name):
+            return psum.tile([P, PACK, P], F32, name=name, tag="work", bufs=7)
 
-        caps = []
+        penalties = []
         for page in range(PAGES):
             page_slots = slots[:, page * COLS : (page + 1) * COLS]
             pos_got = ring.tile([P, PAGE], F32, name="pos_got", align_bytes=64)
             nc.vector.tensor_copy(pos_got[:], pos_pool[:].indirect(page_slots))
+            ahead = bank("ahead")
+            for j in range(PACK):
+                turn(ahead[:, j, :], pos_got[:, j * P : (j + 1) * P], stop=False)
+                turn(ahead[:, j, :], neg_qpos[:].to_broadcast([P, P]), start=False)
             side = ring.tile([P, PACK, P], F32, name="side", align_bytes=64)
-            nc.scalar.activation(
-                side[:].rearrange("q r s -> q s r"),
-                pos_got[:].rearrange("q (s r) -> q s r", r=PACK),
-                ACT.Sign,
-                bias=qpos_col[:],
-                scale=-1.0,
-            )
-            cap = ring.tile([P, PACK, P], F32, name="cap", align_bytes=64)
-            nc.scalar.activation(cap[:], side[:], ACT.Relu, bias=open_col[:], scale=OPEN)
-            caps.append(cap)
+            nc.scalar.activation(side[:], ahead[:], ACT.Sign)
+            penalty = ring.tile([P, PACK, P], F32, name="penalty", align_bytes=64)
+            nc.scalar.activation(penalty[:], side[:], ACT.Relu, scale=OPEN)
+            penalties.append(penalty)
 
-        banks = []
+        negated = keep.tile([P, PAGES, PACK, P], F32, name="negated", align_bytes=64)
+        masked_banks = []
         for page in range(PAGES):
             page_slots = slots[:, page * COLS : (page + 1) * COLS]
             kw_got = ring.tile([P, PAGE], U32, name="kw_got", align_bytes=64)
             nc.vector.tensor_copy(kw_got[:], kw_pool[:].bitcast(U32).indirect(page_slots))
             k_codes = ring.tile([P, PASSES, PAGE], U16, name="k_codes", align_bytes=64)
             nc.vector.tensor_copy(k_codes[:], kw_got[:].bitcast(U16).rearrange("g (n o) -> g o n", o=PASSES))
-            scores = psum.tile([P, PAGE], F32, name="scores", tag="scores", bufs=3)
-            for o in range(PASSES):
-                nc.tensor.matmul_mx(
-                    out=scores[:],
-                    lhsT=q_codes[:, o * NQ : (o + 1) * NQ].bitcast(FP8X4),
-                    lhsT_scale=q_planes[:, o * NQ : (o + 1) * NQ],
-                    rhs=k_codes[:, o, :].bitcast(FP4X4),
-                    rhs_scale=k_planes[:, o * N + page * PAGE : o * N + (page + 1) * PAGE],
-                    start=(o == 0),
-                    stop=(o == PASSES - 1),
-                )
-            banks.append(scores)
+            scores = bank("scores")
+            for j in range(PACK):
+                for o in range(PASSES):
+                    first = o * N + page * PAGE + j * P
+                    nc.tensor.matmul_mx(
+                        out=scores[:, j, :],
+                        lhsT=k_codes[:, o, j * P : (j + 1) * P].bitcast(FP4X4),
+                        lhsT_scale=k_planes[:, first : first + P],
+                        rhs=q_codes[:, o * NQ : (o + 1) * NQ].bitcast(FP8X4),
+                        rhs_scale=q_planes[:, o * NQ : (o + 1) * NQ],
+                        start=(o == 0),
+                        stop=(o == PASSES - 1),
+                    )
+            neg_scores = ring.tile([P, PACK, P], F32, name="neg_scores", align_bytes=64)
+            nc.scalar.activation(neg_scores[:], scores[:], ACT.Copy, scale=-1.0)
+            masked = bank("masked")
+            for j in range(PACK):
+                turn(masked[:, j, :], neg_scores[:, j, :], stop=False)
+                turn(masked[:, j, :], penalties[page][:, j, :], start=False)
+            masked_banks.append(masked)
 
-            if page == PAGES - 1:
-                masked = keep.tile([P, PACK, P], F32, name="masked_last", tag="masked_then_v", align_bytes=64)
-            else:
-                masked = ring.tile([P, PACK, P], F32, name="masked", align_bytes=64)
-            nc.vector.scalar_tensor_tensor(
-                out=masked[:],
-                in0=caps[page][:],
-                scalar=MASKED,
-                in1=scores[:].rearrange("q (s r) -> q r s", r=PACK),
-                op0=ALU.add,
-                op1=ALU.min,
-            )
-            if page == 0:
-                neg_max = keep.tile([P, PAGES], F32, name="neg_max")
-                negated = keep.tile([P, PAGES, PAGE], F32, name="negated", align_bytes=64)
+        def running_min(page, so_far, new):
             nc.vector.tensor_scalar(
-                out=negated[:, page, :],
-                in0=masked[:].rearrange("q r s -> q (r s)"),
-                scalar1=-1.0,
-                scalar2=None if page == 0 else neg_max[:, page - 1 : page],
+                out=negated[:, page, :, :],
+                in0=masked_banks[page][:].rearrange("q j c -> q (j c)").rearrange("q (s r) -> q r s", r=PACK),
+                scalar1=1.0,
+                scalar2=so_far,
                 op0=ALU.mult,
                 op1=ALU.min,
-                accum_out=neg_max[:, page : page + 1],
+                accum_out=new,
             )
 
-        v_codes = keep.tile([P, PAGES * DV], U32, name="v_codes", tag="masked_then_v", align_bytes=64)
+        early_min = keep.tile([P, PAGES - 2], F32, name="early_min")
+        late_min = keep.tile([P, 1], F32, name="late_min", tag="min_then_v", align_bytes=64)
+        running_min(0, None, early_min[:, 0:1])
+        running_min(1, early_min[:, 0:1], early_min[:, 1:2])
+        running_min(2, early_min[:, 1:2], late_min[:])
+
+        vs_cols = keep.tile([P, PAGES, PACK], F32, name="vs_cols", align_bytes=64)
+        for page in range(PAGES):
+            page_slots = slots[:, page * COLS : (page + 1) * COLS]
+            vs_got = ring.tile([P, PAGE], F32, name="vs_got", align_bytes=64)
+            nc.vector.tensor_copy(vs_got[:], vs_pool[:].indirect(page_slots))
+            turned = bank("vs_turned")
+            for r in range(PACK):
+                turn(turned[:, r, :], vs_got[:, r:PAGE:PACK])
+            nc.scalar.copy(vs_cols[:, page, :], turned[:, :, 0])
+
+        neg_max = keep.tile([P, 1], F32, name="neg_max", tag="ks_then_v", align_bytes=64)
+        running_min(3, late_min[:], neg_max[:])
+
+        v_codes = keep.tile([P, PAGES * DV], U32, name="v_codes", tag="min_then_v", align_bytes=64)
         nc.vector.tensor_copy(v_codes[:], vw_pool[:].bitcast(U32).indirect(vcols[:]))
 
         sums = keep.tile([P, PAGES], F32, name="sums")
@@ -192,16 +198,16 @@ def tile_attend_pkv4q_soft_draft_kernel(
         for page in range(PAGES):
             probs = ring.tile([P, PACK, P], F32, name="probs", align_bytes=64)
             nc.scalar.activation(
-                probs[:].rearrange("q r s -> q (r s)"),
-                negated[:, page, :],
+                probs[:],
+                negated[:, page, :, :],
                 ACT.Exp,
-                bias=neg_max[:, PAGES - 1 : PAGES],
+                bias=neg_max[:],
                 scale=-1.0,
                 accum_out=sums[:, page : page + 1],
             )
-            turned = psum.tile([P, PACK, P], F32, name="turned", tag="turned", bufs=PAGES)
+            turned = bank("p_turned")
             for r in range(PACK):
-                nc.tensor.transpose(turned[:, r, :], probs[:, r, :], ident[:])
+                turn(turned[:, r, :], probs[:, r, :])
             weights = ring.tile([P, NQ, PACK], BF16, name="weights", align_bytes=64)
             nc.vector.tensor_tensor(
                 weights[:],

@@ -44,13 +44,12 @@ def tile_attend_pkv4q_soft_draft_kernel(
 
         ks_pool = keep.tile([P, T], U8, name="ks_pool", tag="ks_then_v", align_bytes=64)
         vsc_pool = keep.tile([P, POOL_PAGES * DV], U8, name="vsc_pool", tag="vsc_then_v", align_bytes=64)
-        pos_pool = keep.tile([P, T], F32, name="pos_pool", align_bytes=64)
+        pos_pool = keep.tile([P, T], F32, name="pos_pool", tag="pos_then_v", align_bytes=64)
         kw_pool = keep.tile([P, T], I32, name="kw_pool", align_bytes=64)
         q_codes = keep.tile([P, PASSES * NQ], I32, name="q_codes", align_bytes=64)
         q_planes = keep.tile([P, PASSES * NQ], U8, name="q_planes", align_bytes=64)
         k_planes = keep.tile([P, PASSES * N], U8, name="k_planes", align_bytes=64)
         qpos_col = keep.tile([P, 1], F32, name="qpos_col")
-        neg_qpos = keep.tile([P, 1], F32, name="neg_qpos")
         ident = keep.tile([P, P], F32, name="ident", align_bytes=64)
         warm = keep.tile([P, 1], F32, name="warm")
 
@@ -77,7 +76,6 @@ def tile_attend_pkv4q_soft_draft_kernel(
         nc.gpsimd.dma_start(qpos_col[:], qpos[0])
         make_identity(nc, ident[:])
         nc.scalar.activation(warm[:], ident[:, 0:1], ACT.Exp)
-        nc.scalar.activation(neg_qpos[:], qpos_col[:], ACT.Copy, scale=-1.0)
         nc.gpsimd.dma_start(
             q_codes[:].rearrange("g (o q) -> g o q", o=PASSES),
             q_words[0].rearrange("o g q r -> g o (q r)").bitcast(I32),
@@ -101,7 +99,30 @@ def tile_attend_pkv4q_soft_draft_kernel(
         vs_pool = keep.tile([P, T], F32, name="vs_pool", tag="ks_then_v", align_bytes=64)
         nc.sync.dma_start(vs_pool[:], vs)
 
-        v_planes = keep.tile([P, PAGES * DV], U8, name="v_planes", align_bytes=64)
+        def turn(bank_part, rows, start=True, stop=True):
+            nc.tensor.matmul(bank_part, rows, ident[:], start=start, stop=stop, is_transpose=True)
+
+        def bank(name, tag, bufs):
+            return psum.tile([P, PACK, P], F32, name=name, tag=tag, bufs=bufs)
+
+        masked_banks = []
+        for page in range(PAGES):
+            page_slots = slots[:, page * COLS : (page + 1) * COLS]
+            pos_got = ring.tile([P, PAGE], F32, name="pos_got", align_bytes=64)
+            nc.vector.tensor_copy(pos_got[:], pos_pool[:].indirect(page_slots))
+            side = ring.tile([P, PAGE], F32, name="side", align_bytes=64)
+            nc.scalar.activation(side[:], pos_got[:], ACT.Sign, bias=qpos_col[:], scale=-1.0)
+            side_turned = bank("side_turned", "short", 2)
+            for j in range(PACK):
+                turn(side_turned[:, j, :], side[:, j * P : (j + 1) * P])
+            penalty = ring.tile([P, PACK, P], F32, name="penalty", align_bytes=64)
+            nc.scalar.activation(penalty[:], side_turned[:], ACT.Relu, scale=-OPEN)
+            masked = bank("masked", "page", PAGES)
+            for j in range(PACK):
+                turn(masked[:, j, :], penalty[:, j, :], start=(j == 0), stop=False)
+            masked_banks.append(masked)
+
+        v_planes = keep.tile([P, PAGES * DV], U8, name="v_planes", tag="pos_then_v", align_bytes=64)
         nc.vector.tensor_copy(v_planes[:], vsc_pool[:].indirect(vcols[:]))
 
         vw_pool = keep.tile([P, POOL_PAGES * DV], I32, name="vw_pool", tag="vsc_then_v", align_bytes=64)
@@ -110,36 +131,14 @@ def tile_attend_pkv4q_soft_draft_kernel(
             v_words.rearrange("u g e r -> g u (e r)").bitcast(I32),
         )
 
-        def turn(bank_part, rows, start=True, stop=True):
-            nc.tensor.matmul(bank_part, rows, ident[:], start=start, stop=stop, is_transpose=True)
-
-        def bank(name):
-            return psum.tile([P, PACK, P], F32, name=name, tag="work", bufs=7)
-
-        penalties = []
-        for page in range(PAGES):
-            page_slots = slots[:, page * COLS : (page + 1) * COLS]
-            pos_got = ring.tile([P, PAGE], F32, name="pos_got", align_bytes=64)
-            nc.vector.tensor_copy(pos_got[:], pos_pool[:].indirect(page_slots))
-            ahead = bank("ahead")
-            for j in range(PACK):
-                turn(ahead[:, j, :], pos_got[:, j * P : (j + 1) * P], stop=False)
-                turn(ahead[:, j, :], neg_qpos[:].to_broadcast([P, P]), start=False)
-            side = ring.tile([P, PACK, P], F32, name="side", align_bytes=64)
-            nc.scalar.activation(side[:], ahead[:], ACT.Sign)
-            penalty = ring.tile([P, PACK, P], F32, name="penalty", align_bytes=64)
-            nc.scalar.activation(penalty[:], side[:], ACT.Relu, scale=OPEN)
-            penalties.append(penalty)
-
         negated = keep.tile([P, PAGES, PACK, P], F32, name="negated", align_bytes=64)
-        masked_banks = []
         for page in range(PAGES):
             page_slots = slots[:, page * COLS : (page + 1) * COLS]
             kw_got = ring.tile([P, PAGE], U32, name="kw_got", align_bytes=64)
             nc.vector.tensor_copy(kw_got[:], kw_pool[:].bitcast(U32).indirect(page_slots))
             k_codes = ring.tile([P, PASSES, PAGE], U16, name="k_codes", align_bytes=64)
             nc.vector.tensor_copy(k_codes[:], kw_got[:].bitcast(U16).rearrange("g (n o) -> g o n", o=PASSES))
-            scores = bank("scores")
+            scores = bank("scores", "short", 2)
             for j in range(PACK):
                 for o in range(PASSES):
                     first = o * N + page * PAGE + j * P
@@ -154,43 +153,40 @@ def tile_attend_pkv4q_soft_draft_kernel(
                     )
             neg_scores = ring.tile([P, PACK, P], F32, name="neg_scores", align_bytes=64)
             nc.scalar.activation(neg_scores[:], scores[:], ACT.Copy, scale=-1.0)
-            masked = bank("masked")
             for j in range(PACK):
-                turn(masked[:, j, :], neg_scores[:, j, :], stop=False)
-                turn(masked[:, j, :], penalties[page][:, j, :], start=False)
-            masked_banks.append(masked)
+                turn(masked_banks[page][:, j, :], neg_scores[:, j, :], start=False, stop=(j == PACK - 1))
 
-        def running_min(page, so_far, new):
-            nc.vector.tensor_scalar(
-                out=negated[:, page, :, :],
-                in0=masked_banks[page][:].rearrange("q j c -> q (j c)").rearrange("q (s r) -> q r s", r=PACK),
-                scalar1=1.0,
-                scalar2=so_far,
-                op0=ALU.mult,
-                op1=ALU.min,
-                accum_out=new,
-            )
-
-        early_min = keep.tile([P, PAGES - 2], F32, name="early_min")
-        late_min = keep.tile([P, 1], F32, name="late_min", tag="min_then_v", align_bytes=64)
-        running_min(0, None, early_min[:, 0:1])
-        running_min(1, early_min[:, 0:1], early_min[:, 1:2])
-        running_min(2, early_min[:, 1:2], late_min[:])
-
-        vs_cols = keep.tile([P, PAGES, PACK], F32, name="vs_cols", align_bytes=64)
+        vs_dealt = keep.tile([P, PACK, P], F32, name="vs_dealt", align_bytes=64)
         for page in range(PAGES):
             page_slots = slots[:, page * COLS : (page + 1) * COLS]
             vs_got = ring.tile([P, PAGE], F32, name="vs_got", align_bytes=64)
             nc.vector.tensor_copy(vs_got[:], vs_pool[:].indirect(page_slots))
-            turned = bank("vs_turned")
-            for r in range(PACK):
-                turn(turned[:, r, :], vs_got[:, r:PAGE:PACK])
-            nc.scalar.copy(vs_cols[:, page, :], turned[:, :, 0])
+            rows = slice(32 * page, 32 * (page + 1))
+            nc.scalar.copy(
+                vs_dealt[rows, :, :].rearrange("k r s -> k s r"),
+                vs_got[rows, :].rearrange("k (s r) -> k s r", r=PACK),
+            )
+        vs_turned = bank("vs_turned", "vs", 1)
+        for r in range(PACK):
+            turn(vs_turned[:, r, :], vs_dealt[:, r, :])
+        vs_cols = keep.tile([P, PAGES, PACK], F32, name="vs_cols", align_bytes=64)
+        nc.scalar.copy(vs_cols[:], vs_turned[:, :, 0:P:32].rearrange("s r g -> s g r"))
 
-        neg_max = keep.tile([P, 1], F32, name="neg_max", tag="ks_then_v", align_bytes=64)
-        running_min(3, late_min[:], neg_max[:])
+        page_min = keep.tile([P, PAGES], F32, name="page_min", tag="ks_then_v", align_bytes=64)
+        for page in range(PAGES):
+            nc.vector.tensor_scalar(
+                out=negated[:, page, :, :],
+                in0=masked_banks[page][:].rearrange("q j c -> q (j c)").rearrange("q (s r) -> q r s", r=PACK),
+                scalar1=1.0,
+                scalar2=None,
+                op0=ALU.mult,
+                op1=ALU.min,
+                accum_out=page_min[:, page : page + 1],
+            )
+        neg_max = keep.tile([P, 1], F32, name="neg_max")
+        nc.vector.tensor_reduce(neg_max[:], page_min[:], AXIS.X, ALU.min)
 
-        v_codes = keep.tile([P, PAGES * DV], U32, name="v_codes", tag="min_then_v", align_bytes=64)
+        v_codes = keep.tile([P, PAGES * DV], U32, name="v_codes", tag="ks_then_v", align_bytes=64)
         nc.vector.tensor_copy(v_codes[:], vw_pool[:].bitcast(U32).indirect(vcols[:]))
 
         sums = keep.tile([P, PAGES], F32, name="sums")
@@ -205,7 +201,7 @@ def tile_attend_pkv4q_soft_draft_kernel(
                 scale=-1.0,
                 accum_out=sums[:, page : page + 1],
             )
-            turned = bank("p_turned")
+            turned = bank("p_turned", "page", PAGES)
             for r in range(PACK):
                 turn(turned[:, r, :], probs[:, r, :])
             weights = ring.tile([P, NQ, PACK], BF16, name="weights", align_bytes=64)

from contextlib import ExitStack

import concourse.mybir as mybir
from concourse.masks import make_identity

F32 = mybir.dt.float32
BF16 = mybir.dt.bfloat16
I32 = mybir.dt.int32
U32 = mybir.dt.uint32
U16 = mybir.dt.uint16
U8 = mybir.dt.uint8
FP8X4 = mybir.dt.float8_e4m3fn_x4
FP4X4 = mybir.dt.float4_e2m1fn_x4
ALU = mybir.AluOpType
ACT = mybir.ActivationFunctionType
AXIS = mybir.AxisListType

P = 128
NQ, N, T, D, DV = 128, 2048, 4096, 1024, 256
PAGE = 512
PAGES = N // PAGE
POOL_PAGES = T // PAGE
PACK = 4
PASSES = D // (P * PACK)
QUADS = 4
COLS = PAGE // 16
OPEN = 2.0 ** 100

FLOPS = 2 * NQ * N * D + 2 * NQ * N * DV


def tile_attend_pkv4q_soft_draft_kernel(
    tc, q_words, q_scales, k_words, k_scales, v_words, v_scales, vs, pos, qpos, offs, voffs, out
):
    nc = tc.nc
    with ExitStack() as ctx:
        lists = ctx.enter_context(tc.tile_pool(name="lists", bufs=1))
        keep = ctx.enter_context(tc.tile_pool(name="keep", bufs=1))
        ring = ctx.enter_context(tc.tile_pool(name="ring", bufs=PAGES))
        psum = ctx.enter_context(tc.psum_pool(name="psum", bufs=1))

        slots = lists.tile([P, N // 16], U16, name="slots")
        vcols = lists.tile([P, PAGES * DV // 16], U16, name="vcols")

        ks_pool = keep.tile([P, T], U8, name="ks_pool", tag="ks_then_v", align_bytes=64)
        vsc_pool = keep.tile([P, POOL_PAGES * DV], U8, name="vsc_pool", tag="vsc_then_v", align_bytes=64)
        pos_pool = keep.tile([P, T], F32, name="pos_pool", tag="pos_then_v", align_bytes=64)
        kw_pool = keep.tile([P, T], I32, name="kw_pool", align_bytes=64)
        q_codes = keep.tile([P, PASSES * NQ], I32, name="q_codes", align_bytes=64)
        q_planes = keep.tile([P, PASSES * NQ], U8, name="q_planes", align_bytes=64)
        k_planes = keep.tile([P, PASSES * N], U8, name="k_planes", align_bytes=64)
        qpos_col = keep.tile([P, 1], F32, name="qpos_col")
        ident = keep.tile([P, P], F32, name="ident", align_bytes=64)
        warm = keep.tile([P, 1], F32, name="warm")

        ks_row0 = P - PASSES * 16
        nc.sync.dma_start(slots[:], offs)
        nc.sync.dma_start(
            ks_pool[ks_row0:P, :].bitcast(I32), k_scales.rearrange("o f t -> (o f) t").bitcast(I32)
        )
        nc.sync.dma_start(vcols[:], voffs)
        nc.sync.dma_start(pos_pool[:], pos)
        nc.sync.dma_start(kw_pool[:], k_words[0].rearrange("p t b -> p (t b)").bitcast(I32))

        nc.vector.memset(vsc_pool[:].bitcast(I32), 0)
        nc.vector.memset(ks_pool[0:ks_row0, :].bitcast(I32), 0)
        nc.vector.memset(q_planes[:].bitcast(I32), 0)
        nc.vector.memset(k_planes[:].bitcast(I32), 0)

        for quad in range(QUADS):
            nc.scalar.dma_start(
                vsc_pool[32 * quad : 32 * quad + 4, :].bitcast(I32).rearrange("f (u e) -> f u e", u=POOL_PAGES),
                v_scales[:, 4 * quad : 4 * quad + 4, :].bitcast(I32).rearrange("u f e -> f u e"),
            )

        nc.gpsimd.dma_start(qpos_col[:], qpos[0])
        make_identity(nc, ident[:])
        nc.scalar.activation(warm[:], ident[:, 0:1], ACT.Exp)
        nc.gpsimd.dma_start(
            q_codes[:].rearrange("g (o q) -> g o q", o=PASSES),
            q_words[0].rearrange("o g q r -> g o (q r)").bitcast(I32),
        )
        for quad in range(QUADS):
            nc.gpsimd.dma_start(
                q_planes[32 * quad : 32 * quad + 4, :].bitcast(I32).rearrange("f (o q) -> f o q", o=PASSES),
                q_scales[0, :, 4 * quad : 4 * quad + 4, :].bitcast(I32).rearrange("o f q -> f o q"),
            )

        ks_got = keep.tile([P, N], U8, name="ks_got", align_bytes=64)
        nc.vector.tensor_copy(ks_got[:], ks_pool[:].indirect(slots[:]))
        for o in range(PASSES):
            for quad in range(QUADS):
                row = ks_row0 + 16 * o + 4 * quad
                nc.sync.dma_start(
                    k_planes[32 * quad : 32 * quad + 4, o * N : (o + 1) * N].bitcast(I32),
                    ks_got[row : row + 4, :].bitcast(I32),
                )

        vs_pool = keep.tile([P, T], F32, name="vs_pool", tag="ks_then_v", align_bytes=64)
        nc.sync.dma_start(vs_pool[:], vs)

        def turn(bank_part, rows, start=True, stop=True):
            nc.tensor.matmul(bank_part, rows, ident[:], start=start, stop=stop, is_transpose=True)

        def bank(name, tag, bufs):
            return psum.tile([P, PACK, P], F32, name=name, tag=tag, bufs=bufs)

        masked_banks = []
        for page in range(PAGES):
            page_slots = slots[:, page * COLS : (page + 1) * COLS]
            pos_got = ring.tile([P, PAGE], F32, name="pos_got", align_bytes=64)
            nc.vector.tensor_copy(pos_got[:], pos_pool[:].indirect(page_slots))
            side = ring.tile([P, PAGE], F32, name="side", align_bytes=64)
            nc.scalar.activation(side[:], pos_got[:], ACT.Sign, bias=qpos_col[:], scale=-1.0)
            side_turned = bank("side_turned", "short", 2)
            for j in range(PACK):
                turn(side_turned[:, j, :], side[:, j * P : (j + 1) * P])
            penalty = ring.tile([P, PACK, P], F32, name="penalty", align_bytes=64)
            nc.scalar.activation(penalty[:], side_turned[:], ACT.Relu, scale=-OPEN)
            masked = bank("masked", "page", PAGES)
            for j in range(PACK):
                turn(masked[:, j, :], penalty[:, j, :], start=(j == 0), stop=False)
            masked_banks.append(masked)

        v_planes = keep.tile([P, PAGES * DV], U8, name="v_planes", tag="pos_then_v", align_bytes=64)
        nc.vector.tensor_copy(v_planes[:], vsc_pool[:].indirect(vcols[:]))

        vw_pool = keep.tile([P, POOL_PAGES * DV], I32, name="vw_pool", tag="vsc_then_v", align_bytes=64)
        nc.sync.dma_start(
            vw_pool[:].rearrange("g (u e) -> g u e", u=POOL_PAGES),
            v_words.rearrange("u g e r -> g u (e r)").bitcast(I32),
        )

        negated = keep.tile([P, PAGES, PACK, P], F32, name="negated", align_bytes=64)
        for page in range(PAGES):
            page_slots = slots[:, page * COLS : (page + 1) * COLS]
            kw_got = ring.tile([P, PAGE], U32, name="kw_got", align_bytes=64)
            nc.vector.tensor_copy(kw_got[:], kw_pool[:].bitcast(U32).indirect(page_slots))
            k_codes = ring.tile([P, PASSES, PAGE], U16, name="k_codes", align_bytes=64)
            nc.vector.tensor_copy(k_codes[:], kw_got[:].bitcast(U16).rearrange("g (n o) -> g o n", o=PASSES))
            scores = bank("scores", "short", 2)
            for j in range(PACK):
                for o in range(PASSES):
                    first = o * N + page * PAGE + j * P
                    nc.tensor.matmul_mx(
                        out=scores[:, j, :],
                        lhsT=k_codes[:, o, j * P : (j + 1) * P].bitcast(FP4X4),
                        lhsT_scale=k_planes[:, first : first + P],
                        rhs=q_codes[:, o * NQ : (o + 1) * NQ].bitcast(FP8X4),
                        rhs_scale=q_planes[:, o * NQ : (o + 1) * NQ],
                        start=(o == 0),
                        stop=(o == PASSES - 1),
                    )
            neg_scores = ring.tile([P, PACK, P], F32, name="neg_scores", align_bytes=64)
            nc.scalar.activation(neg_scores[:], scores[:], ACT.Copy, scale=-1.0)
            for j in range(PACK):
                turn(masked_banks[page][:, j, :], neg_scores[:, j, :], start=False, stop=(j == PACK - 1))

        vs_dealt = keep.tile([P, PACK, P], F32, name="vs_dealt", align_bytes=64)
        for page in range(PAGES):
            page_slots = slots[:, page * COLS : (page + 1) * COLS]
            vs_got = ring.tile([P, PAGE], F32, name="vs_got", align_bytes=64)
            nc.vector.tensor_copy(vs_got[:], vs_pool[:].indirect(page_slots))
            rows = slice(32 * page, 32 * (page + 1))
            nc.scalar.copy(
                vs_dealt[rows, :, :].rearrange("k r s -> k s r"),
                vs_got[rows, :].rearrange("k (s r) -> k s r", r=PACK),
            )
        vs_turned = bank("vs_turned", "vs", 1)
        for r in range(PACK):
            turn(vs_turned[:, r, :], vs_dealt[:, r, :])
        vs_cols = keep.tile([P, PAGES, PACK], F32, name="vs_cols", align_bytes=64)
        nc.scalar.copy(vs_cols[:], vs_turned[:, :, 0:P:32].rearrange("s r g -> s g r"))

        page_min = keep.tile([P, PAGES], F32, name="page_min", tag="ks_then_v", align_bytes=64)
        for page in range(PAGES):
            nc.vector.tensor_scalar(
                out=negated[:, page, :, :],
                in0=masked_banks[page][:].rearrange("q j c -> q (j c)").rearrange("q (s r) -> q r s", r=PACK),
                scalar1=1.0,
                scalar2=None,
                op0=ALU.mult,
                op1=ALU.min,
                accum_out=page_min[:, page : page + 1],
            )
        neg_max = keep.tile([P, 1], F32, name="neg_max")
        nc.vector.tensor_reduce(neg_max[:], page_min[:], AXIS.X, ALU.min)

        v_codes = keep.tile([P, PAGES * DV], U32, name="v_codes", tag="ks_then_v", align_bytes=64)
        nc.vector.tensor_copy(v_codes[:], vw_pool[:].bitcast(U32).indirect(vcols[:]))

        sums = keep.tile([P, PAGES], F32, name="sums")
        acc = psum.tile([P, DV], F32, name="acc", tag="acc")
        for page in range(PAGES):
            probs = ring.tile([P, PACK, P], F32, name="probs", align_bytes=64)
            nc.scalar.activation(
                probs[:],
                negated[:, page, :, :],
                ACT.Exp,
                bias=neg_max[:],
                scale=-1.0,
                accum_out=sums[:, page : page + 1],
            )
            turned = bank("p_turned", "page", PAGES)
            for r in range(PACK):
                turn(turned[:, r, :], probs[:, r, :])
            weights = ring.tile([P, NQ, PACK], BF16, name="weights", align_bytes=64)
            nc.vector.tensor_tensor(
                weights[:],
                turned[:].rearrange("s r q -> s q r"),
                vs_cols[:, page, :].unsqueeze(1).broadcast_to([P, NQ, PACK]),
                ALU.mult,
            )
            w_codes = ring.tile([P, NQ], U32, name="w_codes", align_bytes=64)
            w_plane = ring.tile([P, NQ], U8, name="w_plane", align_bytes=64)
            nc.vector.quantize_mx(
                out=w_codes[:].bitcast(FP8X4),
                scales=w_plane[:],
                in_=weights[:].rearrange("s q r -> s (q r)"),
            )
            nc.tensor.matmul_mx(
                out=acc[:],
                lhsT=w_codes[:].bitcast(FP8X4),
                lhsT_scale=w_plane[:],
                rhs=v_codes[:, page * DV : (page + 1) * DV].bitcast(FP8X4),
                rhs_scale=v_planes[:, page * DV : (page + 1) * DV],
                start=(page == 0),
                stop=(page == PAGES - 1),
            )

        total = keep.tile([P, 1], F32, name="total")
        nc.vector.tensor_reduce(total[:], sums[:], AXIS.X, ALU.add)
        inverse = keep.tile([P, 1], F32, name="inverse")
        nc.vector.reciprocal(inverse[:], total[:])
        result = keep.tile([P, DV], F32, name="result", align_bytes=64)
        nc.scalar.activation(result[:], acc[:], ACT.Copy, scale=inverse[:])
        nc.sync.dma_start(out[0], result[:])
